import numpy as np
import ml_dtypes


def mxq(x, axis, fmt="e4m3"):
    dtype, down = {"e4m3": (ml_dtypes.float8_e4m3fn, 7), "e5m2": (ml_dtypes.float8_e5m2, 14)}[fmt]
    v = np.moveaxis(np.asarray(x, np.float32).astype(ml_dtypes.bfloat16).astype(np.float64), axis, -1)
    blocks = v.reshape(v.shape[:-1] + (-1, 32))
    amax = np.abs(blocks).max(-1, keepdims=True)
    byte = np.maximum(np.where(amax > 0, np.frexp(amax)[1] - 1 + 127, 0) - down, 1)
    scale = np.exp2(byte - 127.0)
    codes = (blocks / scale).astype(np.float32).astype(dtype).astype(np.float64)
    return np.moveaxis((codes * scale).reshape(v.shape), -1, axis)


WIDE = False


def mx_kscale(k):
    if not WIDE:
        return np.ones(k)
    levels = np.array([10, -10, 5, -5, 0])
    if k % 512:
        return np.exp2(np.random.permutation(np.resize(levels, k // 32))).repeat(32)
    a = np.empty((k // 512, 16))
    for p in range(k // 512):
        a[p, :8] = np.random.permutation(np.resize(levels, 8))
        for g in range(8):
            far = levels[np.abs(levels - a[p, g]) >= 10]
            a[p, g + 8] = far[np.random.randint(len(far))]
    return np.exp2(a.ravel()).repeat(32)


def f64(x):
    return np.asarray(x).astype(np.float64)


def striped(idx):
    return np.tile(idx.reshape(-1, 16).T, (8, 1)).astype(np.uint16)


def unstriped(offs):
    return offs[:16].T.reshape(-1).astype(np.int64)


E2M1 = np.array([0.0, 0.5, 1.0, 1.5, 2.0, 3.0, 4.0, 6.0, -0.0, -0.5, -1.0, -1.5, -2.0, -3.0, -4.0, -6.0])


def pack_weight(w, fmt):
    k, n = w.shape
    w = f64(np.asarray(w, np.float32).astype(ml_dtypes.bfloat16)).reshape(k // 32, 32, n)
    amax = np.abs(w).max(1)
    if fmt == "e4m3":
        byte = np.frexp(amax)[1] - 1 + 127 - 7
    else:
        mant, ex = np.frexp(amax / 6.0)
        byte = np.where(mant > 0.5, ex, ex - 1) + 127
    byte = np.clip(np.where(amax > 0, byte, 1), 1, 254)
    scaled = (w * np.exp2(127.0 - byte)[:, None, :]).reshape(k, n).astype(np.float32)
    by_word = np.ascontiguousarray(scaled.reshape(k // 512, 128, 4, n).transpose(0, 1, 3, 2))
    if fmt == "e4m3":
        words = by_word.astype(ml_dtypes.float8_e4m3fn).view(np.uint8)
    else:
        c = by_word.astype(ml_dtypes.float4_e2m1fn).view(np.uint8) & 0xF
        words = (c[..., 0::2] | (c[..., 1::2] << 4)).reshape(k // 512, 128, 2 * n)
    return np.ascontiguousarray(words), np.ascontiguousarray(byte.astype(np.uint8).reshape(k // 512, 16, n))


def unpack_weight(words, scales, fmt):
    g, _, n = scales.shape
    words = np.ascontiguousarray(words).reshape(g, 128, n, -1)
    if fmt == "e4m3":
        vals = words.view(ml_dtypes.float8_e4m3fn).astype(np.float64)
    else:
        nib = np.empty((g, 128, n, 4), np.uint8)
        nib[..., 0::2] = words & 0xF
        nib[..., 1::2] = words >> 4
        vals = E2M1[nib]
    vals = vals * np.repeat(np.exp2(scales.astype(np.float64) - 127.0), 8, axis=1)[..., None]
    return vals.transpose(0, 1, 3, 2).reshape(g * 512, n)


def gelu(v):
    return 0.5 * v * (1.0 + np.tanh(np.sqrt(2.0 / np.pi) * (v + 0.044715 * v**3)))


K, K2, H, N, T, S, T2, P = 1024, 512, 1024, 512, 4096, 1024, 2048, 512


def setup_inputs():
    n = np.random.standard_normal
    s = mx_kscale(K)[:, None]
    s2 = mx_kscale(K2)[:, None]
    u = mx_kscale(H)[:, None]
    tab_words, tab_scales = pack_weight(n((K, T)) * s, "e4m3")
    tab2_words, tab2_scales = pack_weight(n((K2, T2)) * s2, "e4m3")
    w2_words, w2_scales = pack_weight(n((K, H)) / np.sqrt(K) / s * u.T, "e2m1")
    w4_words, w4_scales = pack_weight(n((K2, N)) / np.sqrt(K2) / s2, "e4m3")
    return {
        "tab_words": tab_words, "tab_scales": tab_scales,
        "offs": striped(np.random.permutation(T)[:S]),
        "tab2_words": tab2_words, "tab2_scales": tab2_scales,
        "offs2": striped(np.random.permutation(T2)[:P]),
        "pos1": striped(np.random.permutation(S)[:P]),
        "w1": (n((K, H)) / np.sqrt(K) / s * u.T).astype(np.float32),
        "b1": (0.5 * n(H) * u[:, 0]).astype(np.float32),
        "w2_words": w2_words, "w2_scales": w2_scales,
        "w3": (0.52 * n((H, N)) / np.sqrt(H) / u).astype(np.float32),
        "w4_words": w4_words, "w4_scales": w4_scales,
    }


def reference(tab_words, tab_scales, offs, tab2_words, tab2_scales, offs2, pos1,
              w1, b1, w2_words, w2_scales, w3, w4_words, w4_scales):
    v = unpack_weight(tab_words, tab_scales, "e4m3")[:, unstriped(offs)]
    v2 = unpack_weight(tab2_words, tab2_scales, "e4m3")[:, unstriped(offs2)]
    w2 = unpack_weight(w2_words, w2_scales, "e2m1")
    w4 = unpack_weight(w4_words, w4_scales, "e4m3")
    first = (mxq(f64(w1), 0, "e4m3").T @ v) + f64(b1)[:, None]
    second = w2.T @ v
    h = np.maximum(first, second)
    y = mxq(f64(w3), 0, "e4m3").T @ mxq(h, 0, "e4m3")
    b = w4.T @ v2
    yp = y[:, unstriped(pos1)]
    return np.cos(yp) * b + yp

@@ -1,0 +1,357 @@
+from contextlib import ExitStack
+
+import concourse.mybir as mybir
+from concourse.masks import make_identity
+
+K, K2, H, N, T, S, T2, PICKS = 1024, 512, 1024, 512, 4096, 1024, 2048, 512
+FLOPS = 2 * (2 * K * H * S + H * N * S + K2 * N * PICKS)
+
+F32 = mybir.dt.float32
+BF16 = mybir.dt.bfloat16
+I32 = mybir.dt.int32
+U32 = mybir.dt.uint32
+U16 = mybir.dt.uint16
+U8 = mybir.dt.uint8
+FP8X4 = mybir.dt.float8_e4m3fn_x4
+FP4X4 = mybir.dt.float4_e2m1fn_x4
+ACT = mybir.ActivationFunctionType
+ALU = mybir.AluOpType
+
+P = 128
+PACK = 4
+K_PASS = P * PACK
+BANK = 512
+
+
+def tile_list_hip_board_scores_kernel(
+    tc, tab_words, tab_scales, offs, tab2_words, tab2_scales, offs2, pos1,
+    w1, b1, w2_words, w2_scales, w3, w4_words, w4_scales, out,
+):
+    nc = tc.nc
+    with ExitStack() as ctx:
+        keep = ctx.enter_context(tc.tile_pool(name="keep", bufs=1))
+        ring = ctx.enter_context(tc.tile_pool(name="ring", bufs=2))
+        psum = ctx.enter_context(tc.psum_pool(name="psum", bufs=4))
+
+        def kept(name, shape, dtype):
+            return keep.tile(shape, dtype, name=name, align_bytes=64)
+
+        def bank_a(name, shape):
+            return psum.tile(shape, F32, name=name, tag="bank_a")
+
+        def bank_b(name, shape):
+            return psum.tile(shape, F32, name=name, tag="bank_b")
+
+        idx = keep.tile([P, S // 16], U16, name="idx")
+        idx2 = keep.tile([P, PICKS // 16], U16, name="idx2")
+        p1 = keep.tile([P, PICKS // 16], U16, name="p1")
+
+        tab_sc = ring.tile([P, T], U8, name="tab_sc", tag="late_table", bufs=1, align_bytes=64)
+        nc.vector.memset(tab_sc[:].bitcast(I32), 0)
+        nc.sync.dma_start(idx[:], offs)
+        nc.sync.dma_start(idx2[:], offs2)
+        nc.sync.dma_start(p1[:], pos1)
+        b1_rows = kept("b1_rows", [P, P], F32)
+        nc.gpsimd.memset(b1_rows[:], 0.0)
+        for b in range(2):
+            nc.sync.dma_start(
+                out=b1_rows[4 * b : 4 * b + 4, :],
+                in_=b1[K_PASS * b : K_PASS * (b + 1)].rearrange("(g t e) -> t g e", t=4, e=8),
+            )
+        ident = kept("ident", [P, P], F32)
+        make_identity(nc, ident[:])
+        bias_ps = bank_a("bias_ps", [P, P])
+        nc.tensor.transpose(bias_ps[:], b1_rows[:], ident[:])
+        bias = kept("bias", [P, 8], F32)
+        nc.scalar.copy(out=bias[:], in_=bias_ps[:, 0:8])
+
+        def staged(name, shape, dtype, tag):
+            return ring.tile(shape, dtype, name=name, tag=tag, bufs=1, align_bytes=64)
+
+        def load_w1(a, b, tag):
+            raw = staged(f"w1_raw{a}{b}", [P, PACK, BANK], F32, tag)
+            rows = w1[K_PASS * a : K_PASS * (a + 1), BANK * b : BANK * (b + 1)]
+            nc.sync.dma_start(out=raw[:], in_=rows.rearrange("(p j) c -> p j c", j=PACK))
+            return raw
+
+        tab_w = {}
+
+        def load_tab(a):
+            if a == 0:
+                tab_w[a] = staged("tab_w0", [P, T], U32, "stage_c")
+            else:
+                tab_w[a] = ring.tile([P, T], U32, name="tab_w1", tag="late_table", bufs=1, align_bytes=64)
+            nc.sync.dma_start(
+                out=tab_w[a][:].bitcast(I32),
+                in_=tab_words[a].rearrange("p t i -> p (t i)").bitcast(I32),
+            )
+
+        w1_raw = {}
+        w1_raw[0, 0] = load_w1(0, 0, "stage_a")
+        w2_raw = kept("w2_raw", [P, 2, 2 * H], U8)
+        nc.sync.dma_start(
+            out=w2_raw[:].bitcast(I32),
+            in_=w2_words.rearrange("a p c -> p a c").bitcast(I32),
+        )
+        nc.sync.dma_start(
+            out=tab_sc[0:P:4, :].bitcast(I32),
+            in_=tab_scales.rearrange("a q t -> q a t").bitcast(I32),
+        )
+
+        w2_sc_raw = kept("w2_sc_raw", [P, 2, H], U8)
+        nc.vector.memset(w2_sc_raw[:].rearrange("p a c -> p (a c)").bitcast(I32), 0)
+        for q in range(4):
+            nc.gpsimd.dma_start(
+                out=w2_sc_raw[32 * q : 32 * q + 4, :, :].bitcast(I32),
+                in_=w2_scales[:, 4 * q : 4 * q + 4, :].rearrange("a r c -> r a c").bitcast(I32),
+            )
+
+        load_tab(0)
+        v_sc_rows = staged("v_sc_rows", [P, S], U8, "stage_b")
+        nc.vector.tensor_copy(v_sc_rows[:], tab_sc[:].indirect(idx[:]))
+        v_sc = kept("v_sc", [P, 2, S], U8)
+        nc.vector.memset(v_sc[:].rearrange("p a c -> p (a c)").bitcast(I32), 0)
+        for q in range(4):
+            nc.sync.dma_start(
+                out=v_sc[32 * q : 32 * q + 4, :, :].bitcast(I32),
+                in_=v_sc_rows[32 * q : 32 * q + 32 : 4, :].bitcast(I32),
+            )
+
+        load_tab(1)
+        w1_raw[1, 0] = load_w1(1, 0, "stage_a")
+        w1_raw[0, 1] = load_w1(0, 1, "stage_b")
+        w1_raw[1, 1] = load_w1(1, 1, "stage_c")
+        tab2_w = ring.tile([P, T2], U32, name="tab2_w", tag="late_table", bufs=1, align_bytes=64)
+        nc.sync.dma_start(
+            out=tab2_w[:].bitcast(I32),
+            in_=tab2_words[0].rearrange("p t i -> p (t i)").bitcast(I32),
+        )
+        w3_raw = []
+        for b in range(2):
+            raw = staged(f"w3_raw{b}", [P, PACK, N], F32, ("stage_a", "stage_b")[b])
+            rows = w3[K_PASS * b : K_PASS * (b + 1), :].rearrange("(g t e) n -> t g e n", t=4, e=8)
+            for t in range(PACK):
+                nc.sync.dma_start(out=raw[:, t, :], in_=rows[t])
+            w3_raw.append(raw)
+        w4_c = staged("w4_c", [P, N], U32, "stage_c")
+        nc.sync.dma_start(
+            out=w4_c[:].bitcast(I32),
+            in_=w4_words[0].rearrange("p c i -> p (c i)").bitcast(I32),
+        )
+        tab2_sc = kept("tab2_sc", [P, T2], U8)
+        w4_sc = kept("w4_sc", [P, N], U8)
+        nc.vector.memset(tab2_sc[:].bitcast(I32), 0)
+        nc.vector.memset(w4_sc[:].bitcast(I32), 0)
+        for q in range(4):
+            nc.gpsimd.dma_start(
+                out=tab2_sc[32 * q : 32 * q + 4, :].bitcast(I32),
+                in_=tab2_scales[0, 4 * q : 4 * q + 4, :].bitcast(I32),
+            )
+        for q in range(4):
+            nc.gpsimd.dma_start(
+                out=w4_sc[32 * q : 32 * q + 4, :].bitcast(I32),
+                in_=w4_scales[0, 4 * q : 4 * q + 4, :].bitcast(I32),
+            )
+
+        v_c = {}
+
+        def gather_v(a, half):
+            v_c[a, half] = kept(f"v_c{a}{half}", [P, BANK], U32)
+            cols = idx[:, 32 * half : 32 * (half + 1)]
+            nc.vector.tensor_copy(v_c[a, half][:], tab_w[a][:].indirect(cols))
+
+        def copy_on(engine, dst, src):
+            if engine == "vector":
+                nc.vector.tensor_copy(out=dst, in_=src)
+            else:
+                nc.scalar.copy(out=dst, in_=src)
+
+        w1_c, w1_sc = {}, {}
+
+        def round_w1(a, b, engines):
+            grouped = ring.tile([P, PACK * BANK], BF16, name=f"w1_bf{a}{b}", tag="grouped", bufs=3, align_bytes=64)
+            by_block = w1_raw[a, b][:].rearrange("p j (g x) -> p j g x", x=32)
+            for t in range(PACK):
+                src = by_block[:, :, :, 8 * t : 8 * t + 8].rearrange("p j g (e i) -> p g e j i", i=4)
+                dst = grouped[:, BANK * t : BANK * (t + 1)].rearrange("p (g e i j) -> p g e j i", e=2, i=4, j=4)
+                copy_on(engines[t], dst, src)
+            return grouped
+
+        def quantise(codes, scales, grouped, first, count):
+            nc.vector.quantize_mx(
+                out=codes[:, first : first + count].bitcast(FP8X4),
+                scales=scales[:, first : first + count],
+                in_=grouped[:, PACK * first : PACK * (first + count)],
+            )
+
+        def quantise_w1(a, b, grouped, pieces):
+            w1_c[a, b] = kept(f"w1_c{a}{b}", [P, BANK], U32)
+            w1_sc[a, b] = kept(f"w1_sc{a}{b}", [P, BANK], U8)
+            width = BANK // pieces
+            for k in range(pieces):
+                quantise(w1_c[a, b], w1_sc[a, b], grouped, width * k, width)
+
+        all_scalar = ["scalar"] * 4
+        all_vector = ["vector"] * 4
+        g00 = round_w1(0, 0, all_scalar)
+        quantise_w1(0, 0, g00, 1)
+        gather_v(0, 0)
+        gather_v(0, 1)
+
+        w2_sc = kept("w2_sc", [P, 4, PACK, P], U8)
+        nc.vector.tensor_copy(
+            out=w2_sc[:].bitcast(I32).rearrange("p x t (g w) -> p x t g w", w=2),
+            in_=w2_sc_raw[:].rearrange("p a c -> p (a c)").bitcast(I32).rearrange("p (x g t w) -> p x t g w", x=4, t=4, w=2),
+        )
+        gather_v(1, 0)
+        w2_c = kept("w2_c", [P, 4, PACK, 2 * P], U8)
+        nc.vector.tensor_copy(
+            out=w2_c[:].bitcast(I32).rearrange("p x t (g w) -> p x t g w", w=4),
+            in_=w2_raw[:].rearrange("p a c -> p (a c)").bitcast(I32).rearrange("p (x g t w) -> p x t g w", x=4, t=4, w=4),
+        )
+        gather_v(1, 1)
+        g10 = round_w1(1, 0, ["vector", "vector", "scalar", "scalar"])
+        quantise_w1(1, 0, g10, 2)
+
+        first_sb = {}
+
+        def first_bank(b, half, t):
+            if t == 0:
+                first_sb[b, half] = ring.tile([P, PACK, BANK], F32, name=f"first{b}{half}", tag="first", bufs=2)
+            acc = bank_a(f"first_ps{b}{half}{t}", [P, BANK])
+            for a in range(2):
+                nc.tensor.matmul_mx(
+                    out=acc[:],
+                    lhsT=w1_c[a, b][:, P * t : P * (t + 1)].bitcast(FP8X4),
+                    lhsT_scale=w1_sc[a, b][:, P * t : P * (t + 1)],
+                    rhs=v_c[a, half][:].bitcast(FP8X4),
+                    rhs_scale=v_sc[:, a, BANK * half : BANK * (half + 1)],
+                    start=(a == 0),
+                    stop=(a == 1),
+                )
+            nc.scalar.activation(
+                out=first_sb[b, half][:, t, :], in_=acc[:], func=ACT.Identity,
+                bias=bias[:, 4 * b + t : 4 * b + t + 1],
+            )
+
+        h_bf, h_c, h_sc = {}, {}, {}
+
+        def second_bank(b, half, q):
+            if q == 0:
+                h_bf[b, half] = ring.tile([P, PACK * BANK], BF16, name=f"h_bf{b}{half}", tag="h_bf", bufs=2, align_bytes=64)
+                h_c[b, half] = kept(f"h_c{b}{half}", [P, BANK], U32)
+                h_sc[b, half] = kept(f"h_sc{b}{half}", [P, BANK], U8)
+            acc = bank_b(f"second_ps{b}{half}{q}", [P, PACK, P])
+            for a in range(2):
+                for t in range(PACK):
+                    nc.tensor.matmul_mx(
+                        out=acc[:, t, :],
+                        lhsT=w2_c[:, 2 * a + b, t, :].bitcast(FP4X4),
+                        lhsT_scale=w2_sc[:, 2 * a + b, t, :],
+                        rhs=v_c[a, half][:, P * q : P * (q + 1)].bitcast(FP8X4),
+                        rhs_scale=v_sc[:, a, BANK * half + P * q : BANK * half + P * (q + 1)],
+                        start=(a == 0 and t == 0),
+                        stop=(a == 1 and t == PACK - 1),
+                    )
+            nc.vector.tensor_tensor(
+                out=h_bf[b, half][:, BANK * q : BANK * (q + 1)].rearrange("p (c i t) -> p c t i", i=4, t=4),
+                in0=acc[:].rearrange("p t (c i) -> p c t i", i=4),
+                in1=first_sb[b, half][:, :, P * q : P * (q + 1)].rearrange("p t (c i) -> p c t i", i=4),
+                op=ALU.max,
+            )
+
+        def quantise_h(b, half, first, count):
+            quantise(h_c[b, half], h_sc[b, half], h_bf[b, half], first, count)
+
+        w3_c, w3_sc = {}, {}
+
+        def round_w3(b, engine):
+            grouped = ring.tile([P, PACK * N], BF16, name=f"w3_bf{b}", tag="grouped", bufs=3, align_bytes=64)
+            for k in range(2):
+                src = w3_raw[b][:, :, 256 * k : 256 * (k + 1)].rearrange("p t (c i) -> p c t i", i=4)
+                dst = grouped[:, 1024 * k : 1024 * (k + 1)].rearrange("p (c i t) -> p c t i", i=4, t=4)
+                copy_on(engine, dst, src)
+            return grouped
+
+        def quantise_w3(b, grouped):
+            w3_c[b] = kept(f"w3_c{b}", [P, N], U32)
+            w3_sc[b] = kept(f"w3_sc{b}", [P, N], U8)
+            quantise(w3_c[b], w3_sc[b], grouped, 0, N)
+
+        y = [kept(f"y{n}", [P, S], F32) for n in range(4)]
+
+        def y_bank(n, half, first, count):
+            acc = bank_a(f"y_ps{n}{half}{first}", [P, count])
+            for b in range(2):
+                nc.tensor.matmul_mx(
+                    out=acc[:],
+                    lhsT=w3_c[b][:, P * n : P * (n + 1)].bitcast(FP8X4),
+                    lhsT_scale=w3_sc[b][:, P * n : P * (n + 1)],
+                    rhs=h_c[b, half][:, first : first + count].bitcast(FP8X4),
+                    rhs_scale=h_sc[b, half][:, first : first + count],
+                    start=(b == 0),
+                    stop=(b == 1),
+                )
+            nc.scalar.copy(out=y[n][:, BANK * half + first : BANK * half + first + count], in_=acc[:])
+
+        for t in range(PACK):
+            first_bank(0, 0, t)
+        for q in range(4):
+            second_bank(0, 0, q)
+            first_bank(0, 1, q)
+        g01 = round_w1(0, 1, all_vector)
+        quantise_h(0, 0, 0, BANK)
+        quantise_w1(0, 1, g01, 1)
+        g11 = round_w1(1, 1, all_scalar)
+        quantise_w1(1, 1, g11, 1)
+        for q in range(4):
+            second_bank(0, 1, q)
+            first_bank(1, 0, q)
+        quantise_h(0, 1, 0, BANK)
+        g30 = round_w3(0, "scalar")
+        quantise_w3(0, g30)
+        for q in range(4):
+            second_bank(1, 0, q)
+            first_bank(1, 1, q)
+        quantise_h(1, 0, 0, BANK)
+        g31 = round_w3(1, "scalar")
+        quantise_w3(1, g31)
+
+        v2_c = kept("v2_c", [P, PICKS], U32)
+        v2_sc = kept("v2_sc", [P, PICKS], U8)
+        nc.vector.tensor_copy(v2_sc[:], tab2_sc[:].indirect(idx2[:]))
+        nc.vector.tensor_copy(v2_c[:], tab2_w[:].indirect(idx2[:]))
+
+        for q in range(4):
+            second_bank(1, 1, q)
+            y_bank(q, 0, 0, BANK)
+            if q % 2 == 1:
+                quantise_h(1, 1, 256 * (q // 2), 256)
+        for k in range(2):
+            for n in range(4):
+                y_bank(n, 1, 256 * k, 256)
+
+        for n in range(4):
+            b_ps = bank_b(f"b_ps{n}", [P, PICKS])
+            nc.tensor.matmul_mx(
+                out=b_ps[:],
+                lhsT=w4_c[:, P * n : P * (n + 1)].bitcast(FP8X4),
+                lhsT_scale=w4_sc[:, P * n : P * (n + 1)],
+                rhs=v2_c[:].bitcast(FP8X4),
+                rhs_scale=v2_sc[:],
+                start=True,
+                stop=True,
+            )
+            yp = ring.tile([P, PICKS], F32, name=f"yp{n}", tag="yp", bufs=4)
+            nc.vector.tensor_copy(yp[:], y[n][:].indirect(p1[:]))
+            sq = ring.tile([P, PICKS], F32, name=f"sq{n}", tag="sq", bufs=2)
+            nc.scalar.activation(out=sq[:], in_=yp[:], func=ACT.Sin, scale=0.5)
+            nc.scalar.activation(out=sq[:], in_=sq[:], func=ACT.Square)
+            res = ring.tile([P, PICKS], F32, name=f"res{n}", tag="res", bufs=4)
+            nc.vector.scalar_tensor_tensor(
+                out=res[:], in0=sq[:], scalar=-0.5, in1=b_ps[:], op0=ALU.add, op1=ALU.mult
+            )
+            nc.vector.scalar_tensor_tensor(
+                out=res[:], in0=res[:], scalar=-2.0, in1=yp[:], op0=ALU.mult, op1=ALU.add
+            )
+            nc.sync.dma_start(out=out[P * n : P * (n + 1), :], in_=res[:])

@@ -1,3 +1,4 @@
+import math
 from contextlib import ExitStack
 
 import concourse.mybir as mybir
@@ -36,6 +37,9 @@ def tile_list_hip_board_scores_kernel(
         def kept(name, shape, dtype):
             return keep.tile(shape, dtype, name=name, align_bytes=64)
 
+        def staged(name, shape, dtype, tag):
+            return ring.tile(shape, dtype, name=name, tag=tag, bufs=1, align_bytes=64)
+
         def bank_a(name, shape):
             return psum.tile(shape, F32, name=name, tag="bank_a")
 
@@ -46,7 +50,7 @@ def tile_list_hip_board_scores_kernel(
         idx2 = keep.tile([P, PICKS // 16], U16, name="idx2")
         p1 = keep.tile([P, PICKS // 16], U16, name="p1")
 
-        tab_sc = ring.tile([P, T], U8, name="tab_sc", tag="late_table", bufs=1, align_bytes=64)
+        tab_sc = staged("tab_sc", [P, T], U8, "late_table")
         nc.vector.memset(tab_sc[:].bitcast(I32), 0)
         nc.sync.dma_start(idx[:], offs)
         nc.sync.dma_start(idx2[:], offs2)
@@ -65,13 +69,13 @@ def tile_list_hip_board_scores_kernel(
         bias = kept("bias", [P, 8], F32)
         nc.scalar.copy(out=bias[:], in_=bias_ps[:, 0:8])
 
-        def staged(name, shape, dtype, tag):
-            return ring.tile(shape, dtype, name=name, tag=tag, bufs=1, align_bytes=64)
-
-        def load_w1(a, b, tag):
+        def load_w1(a, b, tag, pieces=1):
             raw = staged(f"w1_raw{a}{b}", [P, PACK, BANK], F32, tag)
             rows = w1[K_PASS * a : K_PASS * (a + 1), BANK * b : BANK * (b + 1)]
-            nc.sync.dma_start(out=raw[:], in_=rows.rearrange("(p j) c -> p j c", j=PACK))
+            rows = rows.rearrange("(p j) c -> p j c", j=PACK)
+            step = PACK // pieces
+            for j in range(0, PACK, step):
+                nc.sync.dma_start(out=raw[:, j : j + step, :], in_=rows[:, j : j + step, :])
             return raw
 
         tab_w = {}
@@ -80,19 +84,14 @@ def tile_list_hip_board_scores_kernel(
             if a == 0:
                 tab_w[a] = staged("tab_w0", [P, T], U32, "stage_c")
             else:
-                tab_w[a] = ring.tile([P, T], U32, name="tab_w1", tag="late_table", bufs=1, align_bytes=64)
+                tab_w[a] = staged("tab_w1", [P, T], U32, "late_table")
             nc.sync.dma_start(
                 out=tab_w[a][:].bitcast(I32),
                 in_=tab_words[a].rearrange("p t i -> p (t i)").bitcast(I32),
             )
 
         w1_raw = {}
-        w1_raw[0, 0] = load_w1(0, 0, "stage_a")
-        w2_raw = kept("w2_raw", [P, 2, 2 * H], U8)
-        nc.sync.dma_start(
-            out=w2_raw[:].bitcast(I32),
-            in_=w2_words.rearrange("a p c -> p a c").bitcast(I32),
-        )
+        w1_raw[0, 0] = load_w1(0, 0, "stage_a", pieces=2)
         nc.sync.dma_start(
             out=tab_sc[0:P:4, :].bitcast(I32),
             in_=tab_scales.rearrange("a q t -> q a t").bitcast(I32),
@@ -107,6 +106,14 @@ def tile_list_hip_board_scores_kernel(
             )
 
         load_tab(0)
+        tab2_sc = kept("tab2_sc", [P, T2], U8)
+        nc.vector.memset(tab2_sc[:].bitcast(I32), 0)
+        nc.sync.dma_start(out=tab2_sc[0:P:8, :].bitcast(I32), in_=tab2_scales[0].bitcast(I32))
+        w2_raw = kept("w2_raw", [P, 2, 2 * H], U8)
+        nc.sync.dma_start(
+            out=w2_raw[:].bitcast(I32),
+            in_=w2_words.rearrange("a p c -> p a c").bitcast(I32),
+        )
         v_sc_rows = staged("v_sc_rows", [P, S], U8, "stage_b")
         nc.vector.tensor_copy(v_sc_rows[:], tab_sc[:].indirect(idx[:]))
         v_sc = kept("v_sc", [P, 2, S], U8)
@@ -121,7 +128,7 @@ def tile_list_hip_board_scores_kernel(
         w1_raw[1, 0] = load_w1(1, 0, "stage_a")
         w1_raw[0, 1] = load_w1(0, 1, "stage_b")
         w1_raw[1, 1] = load_w1(1, 1, "stage_c")
-        tab2_w = ring.tile([P, T2], U32, name="tab2_w", tag="late_table", bufs=1, align_bytes=64)
+        tab2_w = staged("tab2_w", [P, T2], U32, "late_table")
         nc.sync.dma_start(
             out=tab2_w[:].bitcast(I32),
             in_=tab2_words[0].rearrange("p t i -> p (t i)").bitcast(I32),
@@ -138,15 +145,8 @@ def tile_list_hip_board_scores_kernel(
             out=w4_c[:].bitcast(I32),
             in_=w4_words[0].rearrange("p c i -> p (c i)").bitcast(I32),
         )
-        tab2_sc = kept("tab2_sc", [P, T2], U8)
         w4_sc = kept("w4_sc", [P, N], U8)
-        nc.vector.memset(tab2_sc[:].bitcast(I32), 0)
         nc.vector.memset(w4_sc[:].bitcast(I32), 0)
-        for q in range(4):
-            nc.gpsimd.dma_start(
-                out=tab2_sc[32 * q : 32 * q + 4, :].bitcast(I32),
-                in_=tab2_scales[0, 4 * q : 4 * q + 4, :].bitcast(I32),
-            )
         for q in range(4):
             nc.gpsimd.dma_start(
                 out=w4_sc[32 * q : 32 * q + 4, :].bitcast(I32),
@@ -163,6 +163,8 @@ def tile_list_hip_board_scores_kernel(
         def copy_on(engine, dst, src):
             if engine == "vector":
                 nc.vector.tensor_copy(out=dst, in_=src)
+            elif engine == "gpsimd":
+                nc.gpsimd.tensor_scalar(out=dst, in0=src, scalar1=1.0, scalar2=0.0, op0=ALU.mult, op1=ALU.add)
             else:
                 nc.scalar.copy(out=dst, in_=src)
 
@@ -195,6 +197,15 @@ def tile_list_hip_board_scores_kernel(
         all_vector = ["vector"] * 4
         g00 = round_w1(0, 0, all_scalar)
         quantise_w1(0, 0, g00, 1)
+        v2_sc_rows = kept("v2_sc_rows", [P, PICKS], U8)
+        nc.vector.tensor_copy(v2_sc_rows[:], tab2_sc[:].indirect(idx2[:]))
+        v2_sc = kept("v2_sc", [P, PICKS], U8)
+        nc.vector.memset(v2_sc[:].bitcast(I32), 0)
+        for q in range(4):
+            nc.gpsimd.dma_start(
+                out=v2_sc[32 * q : 32 * q + 4, :].bitcast(I32),
+                in_=v2_sc_rows[32 * q : 32 * q + 32 : 8, :].bitcast(I32),
+            )
         gather_v(0, 0)
         gather_v(0, 1)
 
@@ -217,7 +228,7 @@ def tile_list_hip_board_scores_kernel(
 
         def first_bank(b, half, t):
             if t == 0:
-                first_sb[b, half] = ring.tile([P, PACK, BANK], F32, name=f"first{b}{half}", tag="first", bufs=2)
+                first_sb[b, half] = staged(f"first{b}{half}", [P, PACK, BANK], F32, f"first{half}")
             acc = bank_a(f"first_ps{b}{half}{t}", [P, BANK])
             for a in range(2):
                 nc.tensor.matmul_mx(
@@ -254,9 +265,9 @@ def tile_list_hip_board_scores_kernel(
                         stop=(a == 1 and t == PACK - 1),
                     )
             nc.vector.tensor_tensor(
-                out=h_bf[b, half][:, BANK * q : BANK * (q + 1)].rearrange("p (c i t) -> p c t i", i=4, t=4),
-                in0=acc[:].rearrange("p t (c i) -> p c t i", i=4),
-                in1=first_sb[b, half][:, :, P * q : P * (q + 1)].rearrange("p t (c i) -> p c t i", i=4),
+                out=h_bf[b, half][:, BANK * q : BANK * (q + 1)].rearrange("p (c i t) -> p c t i", i=2, t=4),
+                in0=acc[:].rearrange("p t (c i) -> p c t i", i=2),
+                in1=first_sb[b, half][:, :, P * q : P * (q + 1)].rearrange("p t (c i) -> p c t i", i=2),
                 op=ALU.max,
             )
 
@@ -267,9 +278,9 @@ def tile_list_hip_board_scores_kernel(
 
         def round_w3(b, engine):
             grouped = ring.tile([P, PACK * N], BF16, name=f"w3_bf{b}", tag="grouped", bufs=3, align_bytes=64)
-            for k in range(2):
-                src = w3_raw[b][:, :, 256 * k : 256 * (k + 1)].rearrange("p t (c i) -> p c t i", i=4)
-                dst = grouped[:, 1024 * k : 1024 * (k + 1)].rearrange("p (c i t) -> p c t i", i=4, t=4)
+            for k in range(4):
+                src = w3_raw[b][:, :, 128 * k : 128 * (k + 1)].rearrange("p t (c i) -> p c t i", i=4)
+                dst = grouped[:, 512 * k : 512 * (k + 1)].rearrange("p (c i t) -> p c t i", i=4, t=4)
                 copy_on(engine, dst, src)
             return grouped
 
@@ -296,19 +307,19 @@ def tile_list_hip_board_scores_kernel(
 
         for t in range(PACK):
             first_bank(0, 0, t)
+        g01 = round_w1(0, 1, all_vector)
+        quantise_w1(0, 1, g01, 1)
         for q in range(4):
             second_bank(0, 0, q)
             first_bank(0, 1, q)
-        g01 = round_w1(0, 1, all_vector)
+        g11 = round_w1(1, 1, ["scalar", "scalar", "vector", "vector"])
         quantise_h(0, 0, 0, BANK)
-        quantise_w1(0, 1, g01, 1)
-        g11 = round_w1(1, 1, all_scalar)
         quantise_w1(1, 1, g11, 1)
         for q in range(4):
             second_bank(0, 1, q)
             first_bank(1, 0, q)
         quantise_h(0, 1, 0, BANK)
-        g30 = round_w3(0, "scalar")
+        g30 = round_w3(0, "gpsimd")
         quantise_w3(0, g30)
         for q in range(4):
             second_bank(1, 0, q)
@@ -317,24 +328,22 @@ def tile_list_hip_board_scores_kernel(
         g31 = round_w3(1, "scalar")
         quantise_w3(1, g31)
 
-        v2_c = kept("v2_c", [P, PICKS], U32)
-        v2_sc = kept("v2_sc", [P, PICKS], U8)
-        nc.vector.tensor_copy(v2_sc[:], tab2_sc[:].indirect(idx2[:]))
-        nc.vector.tensor_copy(v2_c[:], tab2_w[:].indirect(idx2[:]))
-
         for q in range(4):
             second_bank(1, 1, q)
             y_bank(q, 0, 0, BANK)
             if q % 2 == 1:
                 quantise_h(1, 1, 256 * (q // 2), 256)
-        for k in range(2):
+        v2_c = staged("v2_c", [P, PICKS], U32, "first1")
+        nc.vector.tensor_copy(v2_c[:], tab2_w[:].indirect(idx2[:]))
+        for first, count in ((0, 256), (256, 256)):
             for n in range(4):
-                y_bank(n, 1, 256 * k, 256)
+                y_bank(n, 1, first, count)
 
+        b_ps = []
         for n in range(4):
-            b_ps = bank_b(f"b_ps{n}", [P, PICKS])
+            b_ps.append(bank_b(f"b_ps{n}", [P, PICKS]))
             nc.tensor.matmul_mx(
-                out=b_ps[:],
+                out=b_ps[n][:],
                 lhsT=w4_c[:, P * n : P * (n + 1)].bitcast(FP8X4),
                 lhsT_scale=w4_sc[:, P * n : P * (n + 1)],
                 rhs=v2_c[:].bitcast(FP8X4),
@@ -342,16 +351,21 @@ def tile_list_hip_board_scores_kernel(
                 start=True,
                 stop=True,
             )
-            yp = ring.tile([P, PICKS], F32, name=f"yp{n}", tag="yp", bufs=4)
-            nc.vector.tensor_copy(yp[:], y[n][:].indirect(p1[:]))
-            sq = ring.tile([P, PICKS], F32, name=f"sq{n}", tag="sq", bufs=2)
-            nc.scalar.activation(out=sq[:], in_=yp[:], func=ACT.Sin, scale=0.5)
-            nc.scalar.activation(out=sq[:], in_=sq[:], func=ACT.Square)
-            res = ring.tile([P, PICKS], F32, name=f"res{n}", tag="res", bufs=4)
+
+        def finish(n, first, count, subtract_on):
+            cols = slice(first, first + count)
+            yp = kept(f"yp{n}_{first}", [P, count], F32)
+            nc.vector.tensor_copy(yp[:], y[n][:].indirect(p1[:, first // 16 : (first + count) // 16]))
+            work = kept(f"work{n}_{first}", [P, count], F32)
+            nc.scalar.activation(out=work[:], in_=yp[:], func=ACT.Sin, scale=0.5)
+            nc.scalar.activation(out=work[:], in_=work[:], func=ACT.Square, scale=math.sqrt(2.0))
             nc.vector.scalar_tensor_tensor(
-                out=res[:], in0=sq[:], scalar=-0.5, in1=b_ps[:], op0=ALU.add, op1=ALU.mult
+                out=work[:], in0=work[:], scalar=-1.0, in1=b_ps[n][:, cols], op0=ALU.add, op1=ALU.mult
             )
-            nc.vector.scalar_tensor_tensor(
-                out=res[:], in0=res[:], scalar=-2.0, in1=yp[:], op0=ALU.mult, op1=ALU.add
-            )
-            nc.sync.dma_start(out=out[P * n : P * (n + 1), :], in_=res[:])
+            subtract_on.tensor_tensor(out=work[:], in0=yp[:], in1=work[:], op=ALU.subtract)
+            nc.sync.dma_start(out=out[P * n : P * (n + 1), cols], in_=work[:])
+
+        finish(0, 0, PICKS, nc.gpsimd)
+        finish(1, 0, PICKS, nc.gpsimd)
+        finish(2, 0, PICKS, nc.vector)
+        finish(3, 0, PICKS, nc.vector)

import math
from contextlib import ExitStack

import concourse.mybir as mybir
from concourse.masks import make_identity

K, K2, H, N, T, S, T2, PICKS = 1024, 512, 1024, 512, 4096, 1024, 2048, 512
FLOPS = 2 * (2 * K * H * S + H * N * S + K2 * N * PICKS)

F32 = mybir.dt.float32
BF16 = mybir.dt.bfloat16
I32 = mybir.dt.int32
U32 = mybir.dt.uint32
U16 = mybir.dt.uint16
U8 = mybir.dt.uint8
FP8X4 = mybir.dt.float8_e4m3fn_x4
FP4X4 = mybir.dt.float4_e2m1fn_x4
ACT = mybir.ActivationFunctionType
ALU = mybir.AluOpType

P = 128
PACK = 4
K_PASS = P * PACK
BANK = 512


def tile_list_hip_board_scores_kernel(
    tc, tab_words, tab_scales, offs, tab2_words, tab2_scales, offs2, pos1,
    w1, b1, w2_words, w2_scales, w3, w4_words, w4_scales, out,
):
    nc = tc.nc
    with ExitStack() as ctx:
        keep = ctx.enter_context(tc.tile_pool(name="keep", bufs=1))
        ring = ctx.enter_context(tc.tile_pool(name="ring", bufs=2))
        psum = ctx.enter_context(tc.psum_pool(name="psum", bufs=4))

        def kept(name, shape, dtype):
            return keep.tile(shape, dtype, name=name, align_bytes=64)

        def staged(name, shape, dtype, tag):
            return ring.tile(shape, dtype, name=name, tag=tag, bufs=1, align_bytes=64)

        def bank_a(name, shape):
            return psum.tile(shape, F32, name=name, tag="bank_a")

        def bank_b(name, shape):
            return psum.tile(shape, F32, name=name, tag="bank_b")

        idx = keep.tile([P, S // 16], U16, name="idx")
        idx2 = keep.tile([P, PICKS // 16], U16, name="idx2")
        p1 = keep.tile([P, PICKS // 16], U16, name="p1")

        tab_sc = staged("tab_sc", [P, T], U8, "late_table")
        nc.vector.memset(tab_sc[:].bitcast(I32), 0)
        nc.sync.dma_start(idx[:], offs)
        nc.sync.dma_start(idx2[:], offs2)
        nc.sync.dma_start(p1[:], pos1)
        b1_rows = kept("b1_rows", [P, P], F32)
        nc.gpsimd.memset(b1_rows[:], 0.0)
        for b in range(2):
            nc.sync.dma_start(
                out=b1_rows[4 * b : 4 * b + 4, :],
                in_=b1[K_PASS * b : K_PASS * (b + 1)].rearrange("(g t e) -> t g e", t=4, e=8),
            )
        ident = kept("ident", [P, P], F32)
        make_identity(nc, ident[:])
        bias_ps = bank_a("bias_ps", [P, P])
        nc.tensor.transpose(bias_ps[:], b1_rows[:], ident[:])
        bias = kept("bias", [P, 8], F32)
        nc.scalar.copy(out=bias[:], in_=bias_ps[:, 0:8])

        def load_w1(a, b, tag, pieces=1):
            raw = staged(f"w1_raw{a}{b}", [P, PACK, BANK], F32, tag)
            rows = w1[K_PASS * a : K_PASS * (a + 1), BANK * b : BANK * (b + 1)]
            rows = rows.rearrange("(p j) c -> p j c", j=PACK)
            step = PACK // pieces
            for j in range(0, PACK, step):
                nc.sync.dma_start(out=raw[:, j : j + step, :], in_=rows[:, j : j + step, :])
            return raw

        tab_w = {}

        def load_tab(a):
            if a == 0:
                tab_w[a] = staged("tab_w0", [P, T], U32, "stage_c")
            else:
                tab_w[a] = staged("tab_w1", [P, T], U32, "late_table")
            nc.sync.dma_start(
                out=tab_w[a][:].bitcast(I32),
                in_=tab_words[a].rearrange("p t i -> p (t i)").bitcast(I32),
            )

        w1_raw = {}
        w1_raw[0, 0] = load_w1(0, 0, "stage_a", pieces=2)
        nc.sync.dma_start(
            out=tab_sc[0:P:4, :].bitcast(I32),
            in_=tab_scales.rearrange("a q t -> q a t").bitcast(I32),
        )

        w2_sc_raw = kept("w2_sc_raw", [P, 2, H], U8)
        nc.vector.memset(w2_sc_raw[:].rearrange("p a c -> p (a c)").bitcast(I32), 0)
        for q in range(4):
            nc.gpsimd.dma_start(
                out=w2_sc_raw[32 * q : 32 * q + 4, :, :].bitcast(I32),
                in_=w2_scales[:, 4 * q : 4 * q + 4, :].rearrange("a r c -> r a c").bitcast(I32),
            )

        load_tab(0)
        tab2_sc = kept("tab2_sc", [P, T2], U8)
        nc.vector.memset(tab2_sc[:].bitcast(I32), 0)
        nc.sync.dma_start(out=tab2_sc[0:P:8, :].bitcast(I32), in_=tab2_scales[0].bitcast(I32))
        w2_raw = kept("w2_raw", [P, 2, 2 * H], U8)
        nc.sync.dma_start(
            out=w2_raw[:].bitcast(I32),
            in_=w2_words.rearrange("a p c -> p a c").bitcast(I32),
        )
        v_sc_rows = staged("v_sc_rows", [P, S], U8, "stage_b")
        nc.vector.tensor_copy(v_sc_rows[:], tab_sc[:].indirect(idx[:]))
        v_sc = kept("v_sc", [P, 2, S], U8)
        nc.vector.memset(v_sc[:].rearrange("p a c -> p (a c)").bitcast(I32), 0)
        for q in range(4):
            nc.sync.dma_start(
                out=v_sc[32 * q : 32 * q + 4, :, :].bitcast(I32),
                in_=v_sc_rows[32 * q : 32 * q + 32 : 4, :].bitcast(I32),
            )

        load_tab(1)
        w1_raw[1, 0] = load_w1(1, 0, "stage_a")
        w1_raw[0, 1] = load_w1(0, 1, "stage_b")
        w1_raw[1, 1] = load_w1(1, 1, "stage_c")
        tab2_w = staged("tab2_w", [P, T2], U32, "late_table")
        nc.sync.dma_start(
            out=tab2_w[:].bitcast(I32),
            in_=tab2_words[0].rearrange("p t i -> p (t i)").bitcast(I32),
        )
        w3_raw = []
        for b in range(2):
            raw = staged(f"w3_raw{b}", [P, PACK, N], F32, ("stage_a", "stage_b")[b])
            rows = w3[K_PASS * b : K_PASS * (b + 1), :].rearrange("(g t e) n -> t g e n", t=4, e=8)
            for t in range(PACK):
                nc.sync.dma_start(out=raw[:, t, :], in_=rows[t])
            w3_raw.append(raw)
        w4_c = staged("w4_c", [P, N], U32, "stage_c")
        nc.sync.dma_start(
            out=w4_c[:].bitcast(I32),
            in_=w4_words[0].rearrange("p c i -> p (c i)").bitcast(I32),
        )
        w4_sc = kept("w4_sc", [P, N], U8)
        nc.vector.memset(w4_sc[:].bitcast(I32), 0)
        for q in range(4):
            nc.gpsimd.dma_start(
                out=w4_sc[32 * q : 32 * q + 4, :].bitcast(I32),
                in_=w4_scales[0, 4 * q : 4 * q + 4, :].bitcast(I32),
            )

        v_c = {}

        def gather_v(a, half):
            v_c[a, half] = kept(f"v_c{a}{half}", [P, BANK], U32)
            cols = idx[:, 32 * half : 32 * (half + 1)]
            nc.vector.tensor_copy(v_c[a, half][:], tab_w[a][:].indirect(cols))

        def copy_on(engine, dst, src):
            if engine == "vector":
                nc.vector.tensor_copy(out=dst, in_=src)
            elif engine == "gpsimd":
                nc.gpsimd.tensor_scalar(out=dst, in0=src, scalar1=1.0, scalar2=0.0, op0=ALU.mult, op1=ALU.add)
            else:
                nc.scalar.copy(out=dst, in_=src)

        w1_c, w1_sc = {}, {}

        def round_w1(a, b, engines):
            grouped = ring.tile([P, PACK * BANK], BF16, name=f"w1_bf{a}{b}", tag="grouped", bufs=3, align_bytes=64)
            by_block = w1_raw[a, b][:].rearrange("p j (g x) -> p j g x", x=32)
            for t in range(PACK):
                src = by_block[:, :, :, 8 * t : 8 * t + 8].rearrange("p j g (e i) -> p g e j i", i=4)
                dst = grouped[:, BANK * t : BANK * (t + 1)].rearrange("p (g e i j) -> p g e j i", e=2, i=4, j=4)
                copy_on(engines[t], dst, src)
            return grouped

        def quantise(codes, scales, grouped, first, count):
            nc.vector.quantize_mx(
                out=codes[:, first : first + count].bitcast(FP8X4),
                scales=scales[:, first : first + count],
                in_=grouped[:, PACK * first : PACK * (first + count)],
            )

        def quantise_w1(a, b, grouped, pieces):
            w1_c[a, b] = kept(f"w1_c{a}{b}", [P, BANK], U32)
            w1_sc[a, b] = kept(f"w1_sc{a}{b}", [P, BANK], U8)
            width = BANK // pieces
            for k in range(pieces):
                quantise(w1_c[a, b], w1_sc[a, b], grouped, width * k, width)

        all_scalar = ["scalar"] * 4
        all_vector = ["vector"] * 4
        g00 = round_w1(0, 0, all_scalar)
        quantise_w1(0, 0, g00, 1)
        v2_sc_rows = kept("v2_sc_rows", [P, PICKS], U8)
        nc.vector.tensor_copy(v2_sc_rows[:], tab2_sc[:].indirect(idx2[:]))
        v2_sc = kept("v2_sc", [P, PICKS], U8)
        nc.vector.memset(v2_sc[:].bitcast(I32), 0)
        for q in range(4):
            nc.gpsimd.dma_start(
                out=v2_sc[32 * q : 32 * q + 4, :].bitcast(I32),
                in_=v2_sc_rows[32 * q : 32 * q + 32 : 8, :].bitcast(I32),
            )
        gather_v(0, 0)
        gather_v(0, 1)

        w2_sc = kept("w2_sc", [P, 4, PACK, P], U8)
        nc.vector.tensor_copy(
            out=w2_sc[:].bitcast(I32).rearrange("p x t (g w) -> p x t g w", w=2),
            in_=w2_sc_raw[:].rearrange("p a c -> p (a c)").bitcast(I32).rearrange("p (x g t w) -> p x t g w", x=4, t=4, w=2),
        )
        gather_v(1, 0)
        w2_c = kept("w2_c", [P, 4, PACK, 2 * P], U8)
        nc.vector.tensor_copy(
            out=w2_c[:].bitcast(I32).rearrange("p x t (g w) -> p x t g w", w=4),
            in_=w2_raw[:].rearrange("p a c -> p (a c)").bitcast(I32).rearrange("p (x g t w) -> p x t g w", x=4, t=4, w=4),
        )
        gather_v(1, 1)
        g10 = round_w1(1, 0, ["vector", "vector", "scalar", "scalar"])
        quantise_w1(1, 0, g10, 2)

        first_sb = {}

        def first_bank(b, half, t):
            if t == 0:
                first_sb[b, half] = staged(f"first{b}{half}", [P, PACK, BANK], F32, f"first{half}")
            acc = bank_a(f"first_ps{b}{half}{t}", [P, BANK])
            for a in range(2):
                nc.tensor.matmul_mx(
                    out=acc[:],
                    lhsT=w1_c[a, b][:, P * t : P * (t + 1)].bitcast(FP8X4),
                    lhsT_scale=w1_sc[a, b][:, P * t : P * (t + 1)],
                    rhs=v_c[a, half][:].bitcast(FP8X4),
                    rhs_scale=v_sc[:, a, BANK * half : BANK * (half + 1)],
                    start=(a == 0),
                    stop=(a == 1),
                )
            nc.scalar.activation(
                out=first_sb[b, half][:, t, :], in_=acc[:], func=ACT.Identity,
                bias=bias[:, 4 * b + t : 4 * b + t + 1],
            )

        h_bf, h_c, h_sc = {}, {}, {}

        def second_bank(b, half, q):
            if q == 0:
                h_bf[b, half] = ring.tile([P, PACK * BANK], BF16, name=f"h_bf{b}{half}", tag="h_bf", bufs=2, align_bytes=64)
                h_c[b, half] = kept(f"h_c{b}{half}", [P, BANK], U32)
                h_sc[b, half] = kept(f"h_sc{b}{half}", [P, BANK], U8)
            acc = bank_b(f"second_ps{b}{half}{q}", [P, PACK, P])
            for a in range(2):
                for t in range(PACK):
                    nc.tensor.matmul_mx(
                        out=acc[:, t, :],
                        lhsT=w2_c[:, 2 * a + b, t, :].bitcast(FP4X4),
                        lhsT_scale=w2_sc[:, 2 * a + b, t, :],
                        rhs=v_c[a, half][:, P * q : P * (q + 1)].bitcast(FP8X4),
                        rhs_scale=v_sc[:, a, BANK * half + P * q : BANK * half + P * (q + 1)],
                        start=(a == 0 and t == 0),
                        stop=(a == 1 and t == PACK - 1),
                    )
            nc.vector.tensor_tensor(
                out=h_bf[b, half][:, BANK * q : BANK * (q + 1)].rearrange("p (c i t) -> p c t i", i=2, t=4),
                in0=acc[:].rearrange("p t (c i) -> p c t i", i=2),
                in1=first_sb[b, half][:, :, P * q : P * (q + 1)].rearrange("p t (c i) -> p c t i", i=2),
                op=ALU.max,
            )

        def quantise_h(b, half, first, count):
            quantise(h_c[b, half], h_sc[b, half], h_bf[b, half], first, count)

        w3_c, w3_sc = {}, {}

        def round_w3(b, engine):
            grouped = ring.tile([P, PACK * N], BF16, name=f"w3_bf{b}", tag="grouped", bufs=3, align_bytes=64)
            for k in range(4):
                src = w3_raw[b][:, :, 128 * k : 128 * (k + 1)].rearrange("p t (c i) -> p c t i", i=4)
                dst = grouped[:, 512 * k : 512 * (k + 1)].rearrange("p (c i t) -> p c t i", i=4, t=4)
                copy_on(engine, dst, src)
            return grouped

        def quantise_w3(b, grouped):
            w3_c[b] = kept(f"w3_c{b}", [P, N], U32)
            w3_sc[b] = kept(f"w3_sc{b}", [P, N], U8)
            quantise(w3_c[b], w3_sc[b], grouped, 0, N)

        y = [kept(f"y{n}", [P, S], F32) for n in range(4)]

        def y_bank(n, half, first, count):
            acc = bank_a(f"y_ps{n}{half}{first}", [P, count])
            for b in range(2):
                nc.tensor.matmul_mx(
                    out=acc[:],
                    lhsT=w3_c[b][:, P * n : P * (n + 1)].bitcast(FP8X4),
                    lhsT_scale=w3_sc[b][:, P * n : P * (n + 1)],
                    rhs=h_c[b, half][:, first : first + count].bitcast(FP8X4),
                    rhs_scale=h_sc[b, half][:, first : first + count],
                    start=(b == 0),
                    stop=(b == 1),
                )
            nc.scalar.copy(out=y[n][:, BANK * half + first : BANK * half + first + count], in_=acc[:])

        for t in range(PACK):
            first_bank(0, 0, t)
        g01 = round_w1(0, 1, all_vector)
        quantise_w1(0, 1, g01, 1)
        for q in range(4):
            second_bank(0, 0, q)
            first_bank(0, 1, q)
        g11 = round_w1(1, 1, ["scalar", "scalar", "vector", "vector"])
        quantise_h(0, 0, 0, BANK)
        quantise_w1(1, 1, g11, 1)
        for q in range(4):
            second_bank(0, 1, q)
            first_bank(1, 0, q)
        quantise_h(0, 1, 0, BANK)
        g30 = round_w3(0, "gpsimd")
        quantise_w3(0, g30)
        for q in range(4):
            second_bank(1, 0, q)
            first_bank(1, 1, q)
        quantise_h(1, 0, 0, BANK)
        g31 = round_w3(1, "scalar")
        quantise_w3(1, g31)

        for q in range(4):
            second_bank(1, 1, q)
            y_bank(q, 0, 0, BANK)
            if q % 2 == 1:
                quantise_h(1, 1, 256 * (q // 2), 256)
        v2_c = staged("v2_c", [P, PICKS], U32, "first1")
        nc.vector.tensor_copy(v2_c[:], tab2_w[:].indirect(idx2[:]))
        for first, count in ((0, 256), (256, 256)):
            for n in range(4):
                y_bank(n, 1, first, count)

        b_ps = []
        for n in range(4):
            b_ps.append(bank_b(f"b_ps{n}", [P, PICKS]))
            nc.tensor.matmul_mx(
                out=b_ps[n][:],
                lhsT=w4_c[:, P * n : P * (n + 1)].bitcast(FP8X4),
                lhsT_scale=w4_sc[:, P * n : P * (n + 1)],
                rhs=v2_c[:].bitcast(FP8X4),
                rhs_scale=v2_sc[:],
                start=True,
                stop=True,
            )

        def finish(n, first, count, subtract_on):
            cols = slice(first, first + count)
            yp = kept(f"yp{n}_{first}", [P, count], F32)
            nc.vector.tensor_copy(yp[:], y[n][:].indirect(p1[:, first // 16 : (first + count) // 16]))
            work = kept(f"work{n}_{first}", [P, count], F32)
            nc.scalar.activation(out=work[:], in_=yp[:], func=ACT.Sin, scale=0.5)
            nc.scalar.activation(out=work[:], in_=work[:], func=ACT.Square, scale=math.sqrt(2.0))
            nc.vector.scalar_tensor_tensor(
                out=work[:], in0=work[:], scalar=-1.0, in1=b_ps[n][:, cols], op0=ALU.add, op1=ALU.mult
            )
            subtract_on.tensor_tensor(out=work[:], in0=yp[:], in1=work[:], op=ALU.subtract)
            nc.sync.dma_start(out=out[P * n : P * (n + 1), cols], in_=work[:])

        finish(0, 0, PICKS, nc.gpsimd)
        finish(1, 0, PICKS, nc.gpsimd)
        finish(2, 0, PICKS, nc.vector)
        finish(3, 0, PICKS, nc.vector)
